import numpy as np
import ml_dtypes


def mxq(x, axis, fmt="e4m3"):
    dtype, down = {"e4m3": (ml_dtypes.float8_e4m3fn, 7), "e5m2": (ml_dtypes.float8_e5m2, 14)}[fmt]
    v = np.moveaxis(np.asarray(x, np.float32).astype(ml_dtypes.bfloat16).astype(np.float64), axis, -1)
    blocks = v.reshape(v.shape[:-1] + (-1, 32))
    amax = np.abs(blocks).max(-1, keepdims=True)
    byte = np.maximum(np.where(amax > 0, np.frexp(amax)[1] - 1 + 127, 0) - down, 1)
    scale = np.exp2(byte - 127.0)
    codes = (blocks / scale).astype(np.float32).astype(dtype).astype(np.float64)
    return np.moveaxis((codes * scale).reshape(v.shape), -1, axis)


WIDE = False


def mx_kscale(k):
    if not WIDE:
        return np.ones(k)
    levels = np.array([10, -10, 5, -5, 0])
    if k % 512:
        return np.exp2(np.random.permutation(np.resize(levels, k // 32))).repeat(32)
    a = np.empty((k // 512, 16))
    for p in range(k // 512):
        a[p, :8] = np.random.permutation(np.resize(levels, 8))
        for g in range(8):
            far = levels[np.abs(levels - a[p, g]) >= 10]
            a[p, g + 8] = far[np.random.randint(len(far))]
    return np.exp2(a.ravel()).repeat(32)


def f64(x):
    return np.asarray(x).astype(np.float64)


def striped(idx):
    return np.tile(idx.reshape(-1, 16).T, (8, 1)).astype(np.uint16)


def unstriped(offs):
    return offs[:16].T.reshape(-1).astype(np.int64)


def pack_weight(w):
    k, n = w.shape
    w = f64(np.asarray(w, np.float32).astype(ml_dtypes.bfloat16)).reshape(k // 32, 32, n)
    amax = np.abs(w).max(1)
    byte = np.clip(np.where(amax > 0, np.frexp(amax)[1] - 1 + 127 - 7, 1), 1, 254)
    scaled = (w * np.exp2(127.0 - byte)[:, None, :]).reshape(k, n).astype(np.float32)
    words = np.ascontiguousarray(scaled.reshape(k // 512, 128, 4, n).transpose(0, 1, 3, 2)).astype(ml_dtypes.float8_e4m3fn).view(np.uint8)
    return words, np.ascontiguousarray(byte.astype(np.uint8).reshape(k // 512, 16, n))


def unpack_weight(words, scales):
    g, p, n, _ = words.shape
    vals = np.ascontiguousarray(words).view(ml_dtypes.float8_e4m3fn).astype(np.float64) * np.repeat(np.exp2(scales.astype(np.float64) - 127.0), 8, axis=1)[..., None]
    return vals.transpose(0, 1, 3, 2).reshape(g * 512, n)


E2M1 = np.array([0.0, 0.5, 1.0, 1.5, 2.0, 3.0, 4.0, 6.0, -0.0, -0.5, -1.0, -1.5, -2.0, -3.0, -4.0, -6.0])


def pack_fp4(w):
    k, n = w.shape
    w = f64(np.asarray(w, np.float32).astype(ml_dtypes.bfloat16)).reshape(k // 32, 32, n)
    amax = np.abs(w).max(1)
    mant, ex = np.frexp(amax / 6.0)
    byte = np.clip(np.where(amax > 0, np.where(mant > 0.5, ex, ex - 1) + 127, 1), 1, 254)
    scaled = (w * np.exp2(127.0 - byte)[:, None, :]).reshape(k, n).astype(np.float32)
    c = np.ascontiguousarray(scaled.reshape(k // 512, 128, 4, n).transpose(0, 1, 3, 2)).astype(ml_dtypes.float4_e2m1fn).view(np.uint8) & 0xF
    words = (c[..., 0::2] | (c[..., 1::2] << 4)).reshape(k // 512, 128, 2 * n)
    return np.ascontiguousarray(words), np.ascontiguousarray(byte.astype(np.uint8).reshape(k // 512, 16, n))


def unpack_fp4(words, scales):
    g, _, n = scales.shape
    words = np.ascontiguousarray(words).reshape(g, 128, n, 2)
    nib = np.empty((g, 128, n, 4), np.uint8)
    nib[..., 0::2] = words & 0xF
    nib[..., 1::2] = words >> 4
    vals = E2M1[nib] * np.repeat(np.exp2(scales.astype(np.float64) - 127.0), 8, axis=1)[..., None]
    return vals.transpose(0, 1, 3, 2).reshape(g * 512, n)


def relu(v):
    return np.maximum(v, 0.0)


K, T, S, D, N, H, V, U = 1024, 2048, 1024, 4, 128, 512, 256, 512


def setup_inputs():
    n = np.random.standard_normal
    s = mx_kscale(K)[:, None]
    u = mx_kscale(H)
    packed_xT = pack_weight(n((K, T)) * s)
    packed_w1 = pack_fp4(n((K, H)) / np.sqrt(K) / s)
    packed_w2 = pack_fp4(n((K, H)) / np.sqrt(K) / s)
    packed_w3 = pack_fp4(n((H, N)) / np.sqrt(H) / u[:, None])
    return {
        "x_words": packed_xT[0],
        "x_scales": packed_xT[1],
        "w1_words": packed_w1[0],
        "w1_scales": packed_w1[1],
        "w2_words": packed_w2[0],
        "w2_scales": packed_w2[1],
        "clm": (n((H, U))).astype(np.float32),
        "unit": (np.random.uniform(0.6, 1.4, (H, 1)) * u[:, None]).astype(np.float32),
        "w3_words": packed_w3[0],
        "w3_scales": packed_w3[1],
        "offs": striped(np.random.permutation(T)[:S]),
        "prv": striped(np.random.permutation(S)),
        "path": striped(np.random.permutation(np.concatenate([np.arange(V), np.random.randint(0, V, U - V)]))),
    }


def reference(x_words, x_scales, w1_words, w1_scales, w2_words, w2_scales, clm, unit, w3_words, w3_scales, offs, prv, path):
    xq = unpack_weight(x_words, x_scales)[:, unstriped(offs)]
    dl = unpack_fp4(w1_words, w1_scales).T @ xq
    pos = np.tanh(dl)
    ds = unpack_fp4(w2_words, w2_scales).T @ xq
    dp = pos[:, unstriped(prv)]
    trd = np.abs(pos - dp)
    pnl = pos * ds - (0.4 * trd)
    term = pnl.reshape(len(pnl), -1, D).sum(axis=2)
    tpp = term[:, unstriped(path)]
    net = tpp - f64(clm)
    hid = f64(unit) * (relu(-1.0 * net) + 0.3 * net)
    return unpack_fp4(w3_words, w3_scales).T @ mxq(hid, 0, "e4m3")

@@ -1,0 +1,309 @@
+from contextlib import ExitStack
+
+import concourse.mybir as mybir
+from concourse.masks import make_identity
+
+K, T, S, D, N, H, V, U = 1024, 2048, 1024, 4, 128, 512, 256, 512
+FLOPS = 2 * (2 * K * H * S + H * N * U)
+
+F32 = mybir.dt.float32
+BF16 = mybir.dt.bfloat16
+I32 = mybir.dt.int32
+U32 = mybir.dt.uint32
+U16 = mybir.dt.uint16
+U8 = mybir.dt.uint8
+FP8X4 = mybir.dt.float8_e4m3fn_x4
+FP4X4 = mybir.dt.float4_e2m1fn_x4
+ALU = mybir.AluOpType
+ACT = mybir.ActivationFunctionType
+AXIS_X = mybir.AxisListType.X
+
+P = 128
+PACK = 4
+PASSES = K // (P * PACK)
+BANK = 512
+DATE_HALVES = S // BANK
+CLAIM_HALF = U // 2
+TERM_WINDOW = V + 32
+LIST_COL = 16
+
+
+def tile_picked_ydeepm_loss_p_kernel(
+    tc, x_words, x_scales, w1_words, w1_scales, w2_words, w2_scales, clm, unit,
+    w3_words, w3_scales, offs, prv, path, out,
+):
+    nc = tc.nc
+    with ExitStack() as ctx:
+        keep = ctx.enter_context(tc.tile_pool(name="keep", bufs=1))
+        work = ctx.enter_context(tc.tile_pool(name="work", bufs=2))
+        psum = ctx.enter_context(tc.psum_pool(name="psum", bufs=1))
+
+        offs_sb = keep.tile([P, S // LIST_COL], U16, name="offs_sb")
+        prv_sb = keep.tile([P, S // LIST_COL], U16, name="prv_sb")
+        path_sb = keep.tile([P, U // LIST_COL], U16, name="path_sb")
+
+        xs_win = keep.tile([P, T], U8, name="xs_win", align_bytes=64)
+        nc.vector.memset(xs_win[:].bitcast(I32), 0)
+        raw = {}
+        for name in ("w1", "w2"):
+            raw_words = keep.tile([P, PASSES, 2 * H], U8, name=name + "_raw_words")
+            raw_scales = keep.tile([P, PASSES, H], U8, name=name + "_raw_scales")
+            raw[name] = (raw_words, raw_scales)
+
+        def load_dates(o):
+            win = keep.tile([P, T], I32, name="xw_win%d" % o, align_bytes=64)
+            nc.sync.dma_start(win[:], x_words[o].rearrange("p c r -> p (c r)").bitcast(I32))
+            return win
+
+        def load_words(name, words):
+            nc.sync.dma_start(raw[name][0][:].bitcast(I32), words.rearrange("o p c -> p o c").bitcast(I32))
+
+        def load_scales(name, scales, clearer, queue):
+            raw_scales = raw[name][1]
+            clearer.memset(raw_scales[:].rearrange("p o c -> p (o c)").bitcast(I32), 0)
+            for q in range(4):
+                queue.dma_start(
+                    raw_scales[32 * q : 32 * q + 4].bitcast(I32),
+                    scales[:, 4 * q : 4 * q + 4, :].rearrange("o r c -> r o c").bitcast(I32),
+                )
+
+        nc.sync.dma_start(offs_sb[:], offs)
+        load_words("w1", w1_words)
+        for q in range(4):
+            nc.sync.dma_start(
+                xs_win[32 * q : 32 * q + 8, :].bitcast(I32),
+                x_scales[:, 4 * q : 4 * q + 4, :].bitcast(I32),
+            )
+        xw_win = [load_dates(o) for o in range(PASSES)]
+        load_scales("w1", w1_scales, nc.vector, nc.sync)
+        load_scales("w2", w2_scales, nc.vector, nc.sync)
+        load_words("w2", w2_words)
+        w1_raw = raw["w1"]
+        w2_raw = raw["w2"]
+        nc.sync.dma_start(prv_sb[:], prv)
+        nc.sync.dma_start(path_sb[:], path)
+        unit_sb = keep.tile([P, PACK], F32, name="unit_sb")
+        nc.sync.dma_start(unit_sb[:], unit.rearrange("(p t) one -> p (t one)", t=PACK))
+        clm_sb = keep.tile([P, PACK, U], F32, name="clm_sb")
+        nc.sync.dma_start(clm_sb[:], clm.rearrange("(p t) r -> p t r", t=PACK))
+        w3w = keep.tile([P, 2 * N], U8, name="w3w", align_bytes=64)
+        nc.sync.dma_start(w3w[:].bitcast(I32), w3_words[0].bitcast(I32))
+        w3s = keep.tile([P, N], U8, name="w3s", align_bytes=64)
+        nc.vector.memset(w3s[:].bitcast(I32), 0)
+        for q in range(4):
+            nc.sync.dma_start(
+                w3s[32 * q : 32 * q + 4, :].bitcast(I32), w3_scales[0, 4 * q : 4 * q + 4, :].bitcast(I32)
+            )
+
+        xs0 = keep.tile([P, S], U8, name="xs0", align_bytes=64)
+        nc.vector.tensor_copy(xs0[:], xs_win[:].indirect(offs_sb[:]))
+        xs1 = keep.tile([P, S], U8, name="xs1", align_bytes=64)
+        nc.vector.memset(xs1[:].bitcast(I32), 0)
+        nc.scalar.dma_start(xs1[0:112, :].bitcast(I32), xs0[4:116, :].bitcast(I32))
+        xs = [xs0, xs1]
+        xw = {}
+        for o in range(PASSES):
+            for h in range(DATE_HALVES):
+                picked = keep.tile([P, BANK], U32, name="xw%d%d" % (o, h), align_bytes=64)
+                cols = slice(h * BANK // LIST_COL, (h + 1) * BANK // LIST_COL)
+                nc.vector.tensor_copy(picked[:], xw_win[o][:].bitcast(U32).indirect(offs_sb[:, cols]))
+                xw[o, h] = picked
+
+        def deal_words(name, raw, t, engine):
+            words = keep.tile([P, PASSES, P, 2], U8, name="%s_words%d" % (name, t), align_bytes=64)
+            engine.tensor_copy(
+                words[:], raw[0][:].rearrange("p o (m t b) -> p o m t b", t=PACK, b=2)[:, :, :, t, :]
+            )
+            return words
+
+        def deal_scales(name, raw, engine):
+            scales = keep.tile([P, PASSES, PACK, P], U8, name="%s_scales" % name, align_bytes=64)
+            for a, b in ((0, 1), (1, 4)):
+                engine.tensor_copy(scales[:, :, a:b, :], raw[1][:].rearrange("p o (m t) -> p o t m", t=PACK)[:, :, a:b, :])
+            return scales
+
+        words1 = {}
+        words2 = {}
+        words1[0] = deal_words("w1", w1_raw, 0, nc.vector)
+        words1[1] = deal_words("w1", w1_raw, 1, nc.vector)
+        words1[2] = deal_words("w1", w1_raw, 2, nc.vector)
+        words1[3] = deal_words("w1", w1_raw, 3, nc.vector)
+        scales1 = deal_scales("w1", w1_raw, nc.gpsimd)
+        scales2 = deal_scales("w2", w2_raw, nc.gpsimd)
+        words2[0] = deal_words("w2", w2_raw, 0, nc.vector)
+        words2[1] = deal_words("w2", w2_raw, 1, nc.gpsimd)
+        words2[2] = deal_words("w2", w2_raw, 2, nc.gpsimd)
+        words2[3] = deal_words("w2", w2_raw, 3, nc.gpsimd)
+        w1 = [(words1[t], scales1[:, :, t, :]) for t in range(PACK)]
+        w2 = [(words2[t], scales2[:, :, t, :]) for t in range(PACK)]
+
+        def product(weight, h, tag, bufs):
+            words, scales = weight
+            acc = psum.tile([P, BANK], F32, name=tag, tag=tag, bufs=bufs)
+            for o in range(PASSES):
+                nc.tensor.matmul_mx(
+                    out=acc[:],
+                    lhsT=words[:, o].rearrange("p m b -> p (m b)").bitcast(FP4X4),
+                    lhsT_scale=scales[:, o, :],
+                    rhs=xw[o, h][:].bitcast(FP8X4),
+                    rhs_scale=xs[o][:, h * BANK : (h + 1) * BANK],
+                    start=(o == 0),
+                    stop=(o == PASSES - 1),
+                )
+            return acc
+
+
+        unit7 = keep.tile([P, PACK], F32, name="unit7")
+        nc.vector.tensor_scalar(unit7[:], unit_sb[:], 0.7, None, ALU.mult)
+        pos = [keep.tile([P, S], F32, name="pos%d" % t) for t in range(PACK)]
+        neg_term = [keep.tile([P, TERM_WINDOW], F32, name="neg_term%d" % t) for t in range(PACK)]
+        trade = [keep.tile([P, S], F32, name="trade%d" % t) for t in range(PACK)]
+        gain = [keep.tile([P, S], F32, name="gain%d" % t) for t in range(PACK)]
+        for t in range(PACK):
+            nc.vector.memset(neg_term[t][:, V:], 0.0)
+
+        def positions(t, h):
+            dl = product(w1[t], h, "dl", 3)
+            nc.scalar.activation(pos[t][:, h * BANK : (h + 1) * BANK], dl[:], ACT.Tanh)
+
+        ident = keep.tile([P, P], F32, name="ident")
+        make_identity(nc, ident[:])
+        back = {}
+
+        def gains(t, h):
+            dates = slice(h * BANK, (h + 1) * BANK)
+            ds = product(w2[t], h, "ds", 3)
+            order = "p (v e d) -> p e v d"
+            nc.vector.tensor_tensor(
+                gain[t][:, dates].rearrange("p (e v d) -> p e v d", e=2, d=2),
+                ds[:].rearrange(order, e=2, d=2), pos[t][:, dates].rearrange(order, e=2, d=2), ALU.mult,
+            )
+
+        def gain_sums(t, copier):
+            turned = psum.tile([P, DATE_HALVES, P], F32, name="turned", tag="turned", bufs=1)
+            for h in range(DATE_HALVES):
+                planes = gain[t][:, h * BANK : (h + 1) * BANK].rearrange("p (e v d) -> p e d v", e=2, d=2)
+                for j in range(D):
+                    nc.tensor.matmul(turned[:, h, :], planes[:, j // 2, j % 2, :], ident[:],
+                                     start=(j == 0), stop=(j == D - 1), is_transpose=True)
+            turned_sb = work.tile([P, DATE_HALVES, P], F32, name="turned_sb", bufs=2)
+            copier(turned_sb[:], turned[:])
+            back[t] = psum.tile([P, V], F32, name="back", tag="back", bufs=1)
+            for h in range(DATE_HALVES):
+                nc.tensor.transpose(back[t][:, h * P : (h + 1) * P], turned_sb[:, h, :], ident[:])
+
+        dp = [keep.tile([P, S], F32, name="dp%d" % t) for t in range(PACK)]
+
+        def gather(on_scalar, dst, src):
+            if on_scalar:
+                nc.scalar.activation(dst, src, ACT.Copy)
+            else:
+                nc.vector.tensor_copy(dst, src)
+
+        def previous(t, a, b, on_scalar):
+            gather(on_scalar, dp[t][:, a:b], pos[t][:].indirect(prv_sb[:, a // LIST_COL : b // LIST_COL]))
+
+        def trades(t, a, b, engine):
+            engine.tensor_tensor(trade[t][:, a:b], pos[t][:, a:b], dp[t][:, a:b], ALU.subtract)
+
+        trade_sum = [keep.tile([P, V], F32, name="trade_sum%d" % t) for t in range(PACK)]
+
+        def trade_sums(t, a, b):
+            nc.vector.tensor_reduce(
+                trade_sum[t][:, a // D : b // D], trade[t][:, a:b].rearrange("p (v d) -> p v d", d=D), AXIS_X, ALU.add,
+                apply_absolute_value=True,
+            )
+
+        def terms(t, a, b):
+            nc.vector.scalar_tensor_tensor(
+                neg_term[t][:, a // D : b // D],
+                trade_sum[t][:, a // D : b // D], 0.4, back[t][:, a // D : b // D], ALU.mult, ALU.subtract,
+            )
+
+        neg_tpp = [keep.tile([P, U], F32, name="neg_tpp%d" % t) for t in range(PACK)]
+        neg_net = [keep.tile([P, U], F32, name="neg_net%d" % t) for t in range(PACK)]
+        risk = [keep.tile([P, U], F32, name="risk%d" % t) for t in range(PACK)]
+        hid = keep.tile([P, PACK, U], BF16, name="hid")
+
+        def paths(t, a, b, on_scalar):
+            gather(on_scalar, neg_tpp[t][:, a:b], neg_term[t][:].indirect(path_sb[:, a // LIST_COL : b // LIST_COL]))
+
+        def nets(t, a, b, engine):
+            engine.tensor_tensor(neg_net[t][:, a:b], neg_tpp[t][:, a:b], clm_sb[:, t, a:b], ALU.add)
+
+        def risks(t, a, b):
+            nc.vector.scalar_tensor_tensor(
+                risk[t][:, a:b], neg_net[t][:, a:b], -0.3 / 0.7, neg_net[t][:, a:b], ALU.mult, ALU.max
+            )
+
+        def hidden(t, a, b, engine):
+            if engine == "S":
+                nc.scalar.activation(hid[:, t, a:b], risk[t][:, a:b], ACT.Copy, scale=unit7[:, t : t + 1])
+            elif engine == "G":
+                nc.gpsimd.tensor_scalar(hid[:, t, a:b], risk[t][:, a:b], unit7[:, t : t + 1], 0.0, ALU.mult, ALU.add)
+            else:
+                nc.vector.tensor_scalar(hid[:, t, a:b], risk[t][:, a:b], unit7[:, t : t + 1], None, ALU.mult)
+
+        def result(c, weave):
+            woven = keep.tile([P, CLAIM_HALF, PACK], BF16, name="woven%d" % c, align_bytes=64)
+            weave(
+                woven[:].rearrange("p (c i) t -> p c t i", i=4),
+                hid[:, :, c * CLAIM_HALF : (c + 1) * CLAIM_HALF].rearrange("p t (c i) -> p c t i", i=4),
+            )
+            codes = keep.tile([P, CLAIM_HALF], U32, name="codes%d" % c, align_bytes=64)
+            scales = keep.tile([P, CLAIM_HALF], U8, name="scales%d" % c, align_bytes=64)
+            nc.vector.quantize_mx(
+                out=codes[:].bitcast(FP8X4), scales=scales[:], in_=woven[:].rearrange("p c t -> p (c t)")
+            )
+            acc = psum.tile([P, CLAIM_HALF], F32, name="res", tag="dl", bufs=3)
+            nc.tensor.matmul_mx(
+                out=acc[:], lhsT=w3w[:].bitcast(FP4X4), lhsT_scale=w3s[:],
+                rhs=codes[:].bitcast(FP8X4), rhs_scale=scales[:], start=True, stop=True,
+            )
+            res = keep.tile([P, CLAIM_HALF], F32, name="res_sb%d" % c)
+            nc.scalar.copy(res[:], acc[:])
+            nc.sync.dma_start(out[:, c * CLAIM_HALF : (c + 1) * CLAIM_HALF], res[:])
+
+        G = nc.gpsimd
+        LAST = PACK - 1
+        positions(0, 0)
+        positions(0, 1)
+        gains(0, 0)
+        previous(0, 0, 512, False)
+        previous(0, 512, 1024, False)
+        for t in range(PACK):
+            if t > 0:
+                previous(t, 0, 512, True)
+                previous(t, 512, 1024, True)
+            if t + 1 < PACK:
+                positions(t + 1, 0)
+                positions(t + 1, 1)
+            trades(t, 0, 512, G)
+            if t < LAST:
+                trades(t, 512, 1024, G)
+        gains(0, 1)
+        for t in range(LAST):
+            gains(t + 1, 0)
+            gains(t + 1, 1)
+            gain_sums(t, nc.vector.tensor_copy)
+            trade_sums(t, 0, 1024)
+            terms(t, 0, 1024)
+        gain_sums(LAST, nc.vector.tensor_copy)
+        trades(LAST, 512, 1024, G)
+        trade_sums(LAST, 0, 512)
+        trade_sums(LAST, 512, 1024)
+        terms(LAST, 0, 1024)
+        for t in range(LAST):
+            paths(t, 0, 256, True)
+            paths(t, 256, 512, True)
+            nets(t, 0, 512, G)
+        paths(LAST, 0, 256, True)
+        paths(LAST, 256, 512, True)
+        for t in range(LAST):
+            risks(t, 0, 512)
+            hidden(t, 0, 512, "S")
+        for c in range(2):
+            nets(LAST, 256 * c, 256 * c + 256, nc.vector)
+            risks(LAST, 256 * c, 256 * c + 256)
+            hidden(LAST, 256 * c, 256 * c + 256, "V")
+            result(c, nc.vector.tensor_copy)

@@ -43,7 +43,7 @@ def tile_picked_ydeepm_loss_p_kernel(
         path_sb = keep.tile([P, U // LIST_COL], U16, name="path_sb")
 
         xs_win = keep.tile([P, T], U8, name="xs_win", align_bytes=64)
-        nc.vector.memset(xs_win[:].bitcast(I32), 0)
+        nc.gpsimd.memset(xs_win[:].bitcast(I32), 0)
         raw = {}
         for name in ("w1", "w2"):
             raw_words = keep.tile([P, PASSES, 2 * H], U8, name=name + "_raw_words")
@@ -69,18 +69,19 @@ def tile_picked_ydeepm_loss_p_kernel(
 
         nc.sync.dma_start(offs_sb[:], offs)
         load_words("w1", w1_words)
+        nc.sync.dma_start(prv_sb[:], prv)
         for q in range(4):
             nc.sync.dma_start(
                 xs_win[32 * q : 32 * q + 8, :].bitcast(I32),
                 x_scales[:, 4 * q : 4 * q + 4, :].bitcast(I32),
             )
-        xw_win = [load_dates(o) for o in range(PASSES)]
+        xw_win = [load_dates(0)]
         load_scales("w1", w1_scales, nc.vector, nc.sync)
+        xw_win.append(load_dates(1))
         load_scales("w2", w2_scales, nc.vector, nc.sync)
         load_words("w2", w2_words)
         w1_raw = raw["w1"]
         w2_raw = raw["w2"]
-        nc.sync.dma_start(prv_sb[:], prv)
         nc.sync.dma_start(path_sb[:], path)
         unit_sb = keep.tile([P, PACK], F32, name="unit_sb")
         nc.sync.dma_start(unit_sb[:], unit.rearrange("(p t) one -> p (t one)", t=PACK))
@@ -128,12 +129,12 @@ def tile_picked_ydeepm_loss_p_kernel(
         words1[1] = deal_words("w1", w1_raw, 1, nc.vector)
         words1[2] = deal_words("w1", w1_raw, 2, nc.vector)
         words1[3] = deal_words("w1", w1_raw, 3, nc.vector)
-        scales1 = deal_scales("w1", w1_raw, nc.gpsimd)
-        scales2 = deal_scales("w2", w2_raw, nc.gpsimd)
+        scales1 = deal_scales("w1", w1_raw, nc.vector)
+        scales2 = deal_scales("w2", w2_raw, nc.vector)
         words2[0] = deal_words("w2", w2_raw, 0, nc.vector)
-        words2[1] = deal_words("w2", w2_raw, 1, nc.gpsimd)
-        words2[2] = deal_words("w2", w2_raw, 2, nc.gpsimd)
-        words2[3] = deal_words("w2", w2_raw, 3, nc.gpsimd)
+        words2[1] = deal_words("w2", w2_raw, 1, nc.vector)
+        words2[2] = deal_words("w2", w2_raw, 2, nc.vector)
+        words2[3] = deal_words("w2", w2_raw, 3, nc.vector)
         w1 = [(words1[t], scales1[:, :, t, :]) for t in range(PACK)]
         w2 = [(words2[t], scales2[:, :, t, :]) for t in range(PACK)]
 
@@ -173,6 +174,9 @@ def tile_picked_ydeepm_loss_p_kernel(
         def gains(t, h):
             dates = slice(h * BANK, (h + 1) * BANK)
             ds = product(w2[t], h, "ds", 3)
+            if t not in (2, 3):
+                nc.vector.tensor_tensor(gain[t][:, dates], ds[:], pos[t][:, dates], ALU.mult)
+                return
             order = "p (v e d) -> p e v d"
             nc.vector.tensor_tensor(
                 gain[t][:, dates].rearrange("p (e v d) -> p e v d", e=2, d=2),
@@ -180,15 +184,20 @@ def tile_picked_ydeepm_loss_p_kernel(
             )
 
         def gain_sums(t, copier):
-            turned = psum.tile([P, DATE_HALVES, P], F32, name="turned", tag="turned", bufs=1)
+            if t not in (2, 3):
+                back[t] = keep.tile([P, V], F32, name="back%d" % t)
+                nc.vector.tensor_reduce(back[t][:], gain[t][:].rearrange("p (v d) -> p v d", d=D), AXIS_X, ALU.add)
+                return
+            bank = psum.tile([P, 2, DATE_HALVES, P], F32, name="turned", tag="turned", bufs=2)
+            turned = bank[:, 0]
             for h in range(DATE_HALVES):
                 planes = gain[t][:, h * BANK : (h + 1) * BANK].rearrange("p (e v d) -> p e d v", e=2, d=2)
                 for j in range(D):
                     nc.tensor.matmul(turned[:, h, :], planes[:, j // 2, j % 2, :], ident[:],
                                      start=(j == 0), stop=(j == D - 1), is_transpose=True)
             turned_sb = work.tile([P, DATE_HALVES, P], F32, name="turned_sb", bufs=2)
-            copier(turned_sb[:], turned[:])
-            back[t] = psum.tile([P, V], F32, name="back", tag="back", bufs=1)
+            copier(turned_sb[:], turned)
+            back[t] = bank[:, 1].rearrange("p h v -> p (h v)")
             for h in range(DATE_HALVES):
                 nc.tensor.transpose(back[t][:, h * P : (h + 1) * P], turned_sb[:, h, :], ident[:])
 
@@ -206,7 +215,7 @@ def tile_picked_ydeepm_loss_p_kernel(
         def trades(t, a, b, engine):
             engine.tensor_tensor(trade[t][:, a:b], pos[t][:, a:b], dp[t][:, a:b], ALU.subtract)
 
-        trade_sum = [keep.tile([P, V], F32, name="trade_sum%d" % t) for t in range(PACK)]
+        trade_sum = [keep.tile([P, V], F32, name="trade_sum%d" % t) for t in range(4)] * (PACK // 4)
 
         def trade_sums(t, a, b):
             nc.vector.tensor_reduce(
@@ -230,6 +239,12 @@ def tile_picked_ydeepm_loss_p_kernel(
 
         def nets(t, a, b, engine):
             engine.tensor_tensor(neg_net[t][:, a:b], neg_tpp[t][:, a:b], clm_sb[:, t, a:b], ALU.add)
+
+        def path_nets(t, a, b):
+            nc.vector.tensor_tensor(
+                neg_net[t][:, a:b], neg_term[t][:].indirect(path_sb[:, a // LIST_COL : b // LIST_COL]),
+                clm_sb[:, t, a:b], ALU.add,
+            )
 
         def risks(t, a, b):
             nc.vector.scalar_tensor_tensor(
@@ -268,20 +283,22 @@ def tile_picked_ydeepm_loss_p_kernel(
         LAST = PACK - 1
         positions(0, 0)
         positions(0, 1)
-        gains(0, 0)
         previous(0, 0, 512, False)
-        previous(0, 512, 1024, False)
+        previous(0, 512, 1024, True)
+        positions(1, 0)
+        positions(1, 1)
+        gains(0, 0)
+        gains(0, 1)
         for t in range(PACK):
             if t > 0:
                 previous(t, 0, 512, True)
                 previous(t, 512, 1024, True)
-            if t + 1 < PACK:
+            if 0 < t < LAST:
                 positions(t + 1, 0)
                 positions(t + 1, 1)
             trades(t, 0, 512, G)
             if t < LAST:
                 trades(t, 512, 1024, G)
-        gains(0, 1)
         for t in range(LAST):
             gains(t + 1, 0)
             gains(t + 1, 1)

@@ -125,11 +125,11 @@ def tile_picked_ydeepm_loss_p_kernel(
 
         words1 = {}
         words2 = {}
-        words1[0] = deal_words("w1", w1_raw, 0, nc.vector)
-        words1[1] = deal_words("w1", w1_raw, 1, nc.vector)
-        words1[2] = deal_words("w1", w1_raw, 2, nc.vector)
-        words1[3] = deal_words("w1", w1_raw, 3, nc.vector)
-        scales1 = deal_scales("w1", w1_raw, nc.vector)
+        words1[0] = deal_words("w1", w1_raw, 0, nc.gpsimd)
+        scales1 = deal_scales("w1", w1_raw, nc.gpsimd)
+        words1[1] = deal_words("w1", w1_raw, 1, nc.gpsimd)
+        words1[2] = deal_words("w1", w1_raw, 2, nc.gpsimd)
+        words1[3] = deal_words("w1", w1_raw, 3, nc.gpsimd)
         scales2 = deal_scales("w2", w2_raw, nc.vector)
         words2[0] = deal_words("w2", w2_raw, 0, nc.vector)
         words2[1] = deal_words("w2", w2_raw, 1, nc.vector)
@@ -164,7 +164,7 @@ def tile_picked_ydeepm_loss_p_kernel(
             nc.vector.memset(neg_term[t][:, V:], 0.0)
 
         def positions(t, h):
-            dl = product(w1[t], h, "dl", 3)
+            dl = product(w1[t], h, "dl", 4)
             nc.scalar.activation(pos[t][:, h * BANK : (h + 1) * BANK], dl[:], ACT.Tanh)
 
         ident = keep.tile([P, P], F32, name="ident")
@@ -173,8 +173,8 @@ def tile_picked_ydeepm_loss_p_kernel(
 
         def gains(t, h):
             dates = slice(h * BANK, (h + 1) * BANK)
-            ds = product(w2[t], h, "ds", 3)
-            if t not in (2, 3):
+            ds = product(w2[t], h, "ds", 2)
+            if t not in (2,3):
                 nc.vector.tensor_tensor(gain[t][:, dates], ds[:], pos[t][:, dates], ALU.mult)
                 return
             order = "p (v e d) -> p e v d"
@@ -184,7 +184,7 @@ def tile_picked_ydeepm_loss_p_kernel(
             )
 
         def gain_sums(t, copier):
-            if t not in (2, 3):
+            if t not in (2,3):
                 back[t] = keep.tile([P, V], F32, name="back%d" % t)
                 nc.vector.tensor_reduce(back[t][:], gain[t][:].rearrange("p (v d) -> p v d", d=D), AXIS_X, ALU.add)
                 return
@@ -215,7 +215,8 @@ def tile_picked_ydeepm_loss_p_kernel(
         def trades(t, a, b, engine):
             engine.tensor_tensor(trade[t][:, a:b], pos[t][:, a:b], dp[t][:, a:b], ALU.subtract)
 
-        trade_sum = [keep.tile([P, V], F32, name="trade_sum%d" % t) for t in range(4)] * (PACK // 4)
+        sums = [keep.tile([P, V], F32, name="trade_sum%d" % t) for t in range(4)]
+        trade_sum = [sums[i] for i in (0,1,2,3)]
 
         def trade_sums(t, a, b):
             nc.vector.tensor_reduce(
@@ -259,68 +260,77 @@ def tile_picked_ydeepm_loss_p_kernel(
             else:
                 nc.vector.tensor_scalar(hid[:, t, a:b], risk[t][:, a:b], unit7[:, t : t + 1], None, ALU.mult)
 
-        def result(c, weave):
-            woven = keep.tile([P, CLAIM_HALF, PACK], BF16, name="woven%d" % c, align_bytes=64)
-            weave(
+        def result(a, b, copier):
+            n = b - a
+            woven = keep.tile([P, n, PACK], BF16, name="woven%d" % a, align_bytes=64)
+            nc.vector.tensor_copy(
                 woven[:].rearrange("p (c i) t -> p c t i", i=4),
-                hid[:, :, c * CLAIM_HALF : (c + 1) * CLAIM_HALF].rearrange("p t (c i) -> p c t i", i=4),
+                hid[:, :, a:b].rearrange("p t (c i) -> p c t i", i=4),
             )
-            codes = keep.tile([P, CLAIM_HALF], U32, name="codes%d" % c, align_bytes=64)
-            scales = keep.tile([P, CLAIM_HALF], U8, name="scales%d" % c, align_bytes=64)
+            codes = keep.tile([P, n], U32, name="codes%d" % a, align_bytes=64)
+            scales = keep.tile([P, n], U8, name="scales%d" % a, align_bytes=64)
             nc.vector.quantize_mx(
                 out=codes[:].bitcast(FP8X4), scales=scales[:], in_=woven[:].rearrange("p c t -> p (c t)")
             )
-            acc = psum.tile([P, CLAIM_HALF], F32, name="res", tag="dl", bufs=3)
+            acc = psum.tile([P, n], F32, name="res", tag="dl", bufs=4)
             nc.tensor.matmul_mx(
                 out=acc[:], lhsT=w3w[:].bitcast(FP4X4), lhsT_scale=w3s[:],
                 rhs=codes[:].bitcast(FP8X4), rhs_scale=scales[:], start=True, stop=True,
             )
-            res = keep.tile([P, CLAIM_HALF], F32, name="res_sb%d" % c)
-            nc.scalar.copy(res[:], acc[:])
-            nc.sync.dma_start(out[:, c * CLAIM_HALF : (c + 1) * CLAIM_HALF], res[:])
+            res = keep.tile([P, n], F32, name="res_sb%d" % a)
+            copier(res[:], acc[:])
+            nc.sync.dma_start(out[:, a:b], res[:])
 
         G = nc.gpsimd
         LAST = PACK - 1
-        positions(0, 0)
-        positions(0, 1)
+        def both(step, t):
+            step(t, 0)
+            step(t, 1)
+        def claims(t):
+            paths(t, 0, 256, (False,True,True)[t])
+            paths(t, 256, 512, True)
+            nets(t, 0, 512, (G,G,nc.vector)[t])
+        def finish(t):
+            risks(t, 0, 512)
+            hidden(t, 0, 512, "SSS"[t])
+        both(positions, 0)
         previous(0, 0, 512, False)
         previous(0, 512, 1024, True)
-        positions(1, 0)
-        positions(1, 1)
-        gains(0, 0)
-        gains(0, 1)
-        for t in range(PACK):
-            if t > 0:
-                previous(t, 0, 512, True)
-                previous(t, 512, 1024, True)
-            if 0 < t < LAST:
-                positions(t + 1, 0)
-                positions(t + 1, 1)
-            trades(t, 0, 512, G)
-            if t < LAST:
-                trades(t, 512, 1024, G)
+        both(positions, 1)
+        both(gains, 0)
         for t in range(LAST):
-            gains(t + 1, 0)
-            gains(t + 1, 1)
-            gain_sums(t, nc.vector.tensor_copy)
+            trades(t, 0, 512, G)
+            trades(t, 512, 1024, G)
+            both(gains, t + 1)
+            gain_sums(t, nc.scalar.copy)
             trade_sums(t, 0, 1024)
             terms(t, 0, 1024)
-        gain_sums(LAST, nc.vector.tensor_copy)
+            previous(t + 1, 0, 512, True)
+            previous(t + 1, 512, 1024, True)
+            if t + 2 < PACK:
+                both(positions, t + 2)
+            if t >= 0:
+                claims(t - 0)
+            if t >= 3:
+                finish(t - 3)
+        gain_sums(LAST, nc.scalar.copy)
+        trades(LAST, 0, 512, G)
         trades(LAST, 512, 1024, G)
         trade_sums(LAST, 0, 512)
         trade_sums(LAST, 512, 1024)
         terms(LAST, 0, 1024)
-        for t in range(LAST):
-            paths(t, 0, 256, True)
-            paths(t, 256, 512, True)
-            nets(t, 0, 512, G)
+        for t in range(max(0, LAST - 0), LAST):
+            claims(t)
         paths(LAST, 0, 256, True)
         paths(LAST, 256, 512, True)
-        for t in range(LAST):
-            risks(t, 0, 512)
-            hidden(t, 0, 512, "S")
+        for t in range(max(0, LAST - 3), LAST):
+            finish(t)
         for c in range(2):
             nets(LAST, 256 * c, 256 * c + 256, nc.vector)
             risks(LAST, 256 * c, 256 * c + 256)
             hidden(LAST, 256 * c, 256 * c + 256, "V")
-            result(c, nc.vector.tensor_copy)
+            if c == 0:
+                result(0, 256, nc.scalar.copy)
+            else:
+                result(256, 384, nc.scalar.copy)
+                result(384, 512, nc.vector.tensor_copy)

@@ -21,11 +21,17 @@ AXIS_X = mybir.AxisListType.X
 P = 128
 PACK = 4
 PASSES = K // (P * PACK)
+QUADRANTS = 4
 BANK = 512
 DATE_HALVES = S // BANK
 CLAIM_HALF = U // 2
-TERM_WINDOW = V + 32
+CLAIM_QUARTER = U // 4
 LIST_COL = 16
+TERM_WINDOW = V + 32
+SHIFT_ROWS = 112
+LAST = PACK - 1
+
+DL_BANKS, DS_BANKS, SUM_BANKS = 4, 2, 2
 
 
 def tile_picked_ydeepm_loss_p_kernel(
@@ -38,121 +44,115 @@ def tile_picked_ydeepm_loss_p_kernel(
         work = ctx.enter_context(tc.tile_pool(name="work", bufs=2))
         psum = ctx.enter_context(tc.psum_pool(name="psum", bufs=1))
 
+        def entries(list_tile, a, b):
+            return list_tile[:, a // LIST_COL : b // LIST_COL]
+
+        def date_half(h):
+            return slice(h * BANK, (h + 1) * BANK)
+
         offs_sb = keep.tile([P, S // LIST_COL], U16, name="offs_sb")
         prv_sb = keep.tile([P, S // LIST_COL], U16, name="prv_sb")
         path_sb = keep.tile([P, U // LIST_COL], U16, name="path_sb")
 
-        xs_win = keep.tile([P, T], U8, name="xs_win", align_bytes=64)
-        nc.gpsimd.memset(xs_win[:].bitcast(I32), 0)
-        raw = {}
-        for name in ("w1", "w2"):
-            raw_words = keep.tile([P, PASSES, 2 * H], U8, name=name + "_raw_words")
-            raw_scales = keep.tile([P, PASSES, H], U8, name=name + "_raw_scales")
-            raw[name] = (raw_words, raw_scales)
+        x_scale_table = keep.tile([P, T], U8, name="x_scale_table", align_bytes=64)
+        nc.gpsimd.memset(x_scale_table[:].bitcast(I32), 0)
+        w1_raw_words = keep.tile([P, PASSES, 2 * H], U8, name="w1_raw_words")
+        w1_raw_scales = keep.tile([P, PASSES, H], U8, name="w1_raw_scales")
+        w2_raw_words = keep.tile([P, PASSES, 2 * H], U8, name="w2_raw_words")
+        w2_raw_scales = keep.tile([P, PASSES, H], U8, name="w2_raw_scales")
 
-        def load_dates(o):
-            win = keep.tile([P, T], I32, name="xw_win%d" % o, align_bytes=64)
-            nc.sync.dma_start(win[:], x_words[o].rearrange("p c r -> p (c r)").bitcast(I32))
-            return win
+        def load_x_words(o):
+            table = keep.tile([P, T], I32, name="x_word_table%d" % o, align_bytes=64)
+            nc.sync.dma_start(table[:], x_words[o].rearrange("p c r -> p (c r)").bitcast(I32))
+            return table
 
-        def load_words(name, words):
-            nc.sync.dma_start(raw[name][0][:].bitcast(I32), words.rearrange("o p c -> p o c").bitcast(I32))
+        def load_weight_words(raw_words, words):
+            nc.sync.dma_start(raw_words[:].bitcast(I32), words.rearrange("o p c -> p o c").bitcast(I32))
 
-        def load_scales(name, scales, clearer, queue):
-            raw_scales = raw[name][1]
-            clearer.memset(raw_scales[:].rearrange("p o c -> p (o c)").bitcast(I32), 0)
-            for q in range(4):
-                queue.dma_start(
+        def load_weight_scales(raw_scales, scales):
+            nc.vector.memset(raw_scales[:].rearrange("p o c -> p (o c)").bitcast(I32), 0)
+            for q in range(QUADRANTS):
+                nc.sync.dma_start(
                     raw_scales[32 * q : 32 * q + 4].bitcast(I32),
                     scales[:, 4 * q : 4 * q + 4, :].rearrange("o r c -> r o c").bitcast(I32),
                 )
 
         nc.sync.dma_start(offs_sb[:], offs)
-        load_words("w1", w1_words)
+        load_weight_words(w1_raw_words, w1_words)
         nc.sync.dma_start(prv_sb[:], prv)
-        for q in range(4):
+        for q in range(QUADRANTS):
             nc.sync.dma_start(
-                xs_win[32 * q : 32 * q + 8, :].bitcast(I32),
+                x_scale_table[32 * q : 32 * q + 8, :].bitcast(I32),
                 x_scales[:, 4 * q : 4 * q + 4, :].bitcast(I32),
             )
-        xw_win = [load_dates(0)]
-        load_scales("w1", w1_scales, nc.vector, nc.sync)
-        xw_win.append(load_dates(1))
-        load_scales("w2", w2_scales, nc.vector, nc.sync)
-        load_words("w2", w2_words)
-        w1_raw = raw["w1"]
-        w2_raw = raw["w2"]
+        x_word_tables = [load_x_words(0)]
+        load_weight_scales(w1_raw_scales, w1_scales)
+        x_word_tables.append(load_x_words(1))
+        load_weight_scales(w2_raw_scales, w2_scales)
+        load_weight_words(w2_raw_words, w2_words)
         nc.sync.dma_start(path_sb[:], path)
         unit_sb = keep.tile([P, PACK], F32, name="unit_sb")
         nc.sync.dma_start(unit_sb[:], unit.rearrange("(p t) one -> p (t one)", t=PACK))
         clm_sb = keep.tile([P, PACK, U], F32, name="clm_sb")
         nc.sync.dma_start(clm_sb[:], clm.rearrange("(p t) r -> p t r", t=PACK))
-        w3w = keep.tile([P, 2 * N], U8, name="w3w", align_bytes=64)
-        nc.sync.dma_start(w3w[:].bitcast(I32), w3_words[0].bitcast(I32))
-        w3s = keep.tile([P, N], U8, name="w3s", align_bytes=64)
-        nc.vector.memset(w3s[:].bitcast(I32), 0)
-        for q in range(4):
+        w3_words_sb = keep.tile([P, 2 * N], U8, name="w3_words_sb", align_bytes=64)
+        nc.sync.dma_start(w3_words_sb[:].bitcast(I32), w3_words[0].bitcast(I32))
+        w3_scales_sb = keep.tile([P, N], U8, name="w3_scales_sb", align_bytes=64)
+        nc.vector.memset(w3_scales_sb[:].bitcast(I32), 0)
+        for q in range(QUADRANTS):
             nc.sync.dma_start(
-                w3s[32 * q : 32 * q + 4, :].bitcast(I32), w3_scales[0, 4 * q : 4 * q + 4, :].bitcast(I32)
+                w3_scales_sb[32 * q : 32 * q + 4, :].bitcast(I32),
+                w3_scales[0, 4 * q : 4 * q + 4, :].bitcast(I32),
             )
 
-        xs0 = keep.tile([P, S], U8, name="xs0", align_bytes=64)
-        nc.vector.tensor_copy(xs0[:], xs_win[:].indirect(offs_sb[:]))
-        xs1 = keep.tile([P, S], U8, name="xs1", align_bytes=64)
-        nc.vector.memset(xs1[:].bitcast(I32), 0)
-        nc.scalar.dma_start(xs1[0:112, :].bitcast(I32), xs0[4:116, :].bitcast(I32))
-        xs = [xs0, xs1]
-        xw = {}
+        picked_scales0 = keep.tile([P, S], U8, name="picked_scales0", align_bytes=64)
+        nc.vector.tensor_copy(picked_scales0[:], x_scale_table[:].indirect(offs_sb[:]))
+        picked_scales1 = keep.tile([P, S], U8, name="picked_scales1", align_bytes=64)
+        nc.vector.memset(picked_scales1[:].bitcast(I32), 0)
+        nc.scalar.dma_start(
+            picked_scales1[0:SHIFT_ROWS, :].bitcast(I32), picked_scales0[4 : 4 + SHIFT_ROWS, :].bitcast(I32)
+        )
+        picked_scales = [picked_scales0, picked_scales1]
+        picked_words = {}
         for o in range(PASSES):
             for h in range(DATE_HALVES):
-                picked = keep.tile([P, BANK], U32, name="xw%d%d" % (o, h), align_bytes=64)
-                cols = slice(h * BANK // LIST_COL, (h + 1) * BANK // LIST_COL)
-                nc.vector.tensor_copy(picked[:], xw_win[o][:].bitcast(U32).indirect(offs_sb[:, cols]))
-                xw[o, h] = picked
+                picked = keep.tile([P, BANK], U32, name="picked_words%d%d" % (o, h), align_bytes=64)
+                table = x_word_tables[o][:].bitcast(U32)
+                nc.vector.tensor_copy(picked[:], table.indirect(entries(offs_sb, h * BANK, (h + 1) * BANK)))
+                picked_words[o, h] = picked
 
-        def deal_words(name, raw, t, engine):
+        def deal_words(name, raw_words, t, engine):
             words = keep.tile([P, PASSES, P, 2], U8, name="%s_words%d" % (name, t), align_bytes=64)
-            engine.tensor_copy(
-                words[:], raw[0][:].rearrange("p o (m t b) -> p o m t b", t=PACK, b=2)[:, :, :, t, :]
-            )
+            columns = raw_words[:].rearrange("p o (m t b) -> p o m t b", t=PACK, b=2)
+            engine.tensor_copy(words[:], columns[:, :, :, t, :])
             return words
 
-        def deal_scales(name, raw, engine):
+        def deal_scales(name, raw_scales, engine):
             scales = keep.tile([P, PASSES, PACK, P], U8, name="%s_scales" % name, align_bytes=64)
-            for a, b in ((0, 1), (1, 4)):
-                engine.tensor_copy(scales[:, :, a:b, :], raw[1][:].rearrange("p o (m t) -> p o t m", t=PACK)[:, :, a:b, :])
+            columns = raw_scales[:].rearrange("p o (m t) -> p o t m", t=PACK)
+            for a, b in ((0, 1), (1, PACK)):
+                engine.tensor_copy(scales[:, :, a:b, :], columns[:, :, a:b, :])
             return scales
 
-        words1 = {}
-        words2 = {}
-        words1[0] = deal_words("w1", w1_raw, 0, nc.gpsimd)
-        scales1 = deal_scales("w1", w1_raw, nc.gpsimd)
-        words1[1] = deal_words("w1", w1_raw, 1, nc.gpsimd)
-        words1[2] = deal_words("w1", w1_raw, 2, nc.gpsimd)
-        words1[3] = deal_words("w1", w1_raw, 3, nc.gpsimd)
-        scales2 = deal_scales("w2", w2_raw, nc.vector)
-        words2[0] = deal_words("w2", w2_raw, 0, nc.vector)
-        words2[1] = deal_words("w2", w2_raw, 1, nc.vector)
-        words2[2] = deal_words("w2", w2_raw, 2, nc.vector)
-        words2[3] = deal_words("w2", w2_raw, 3, nc.vector)
-        w1 = [(words1[t], scales1[:, :, t, :]) for t in range(PACK)]
-        w2 = [(words2[t], scales2[:, :, t, :]) for t in range(PACK)]
+        w1_dealt_words = [deal_words("w1", w1_raw_words, 0, nc.gpsimd)]
+        w1_dealt_scales = deal_scales("w1", w1_raw_scales, nc.gpsimd)
+        w1_dealt_words.extend(deal_words("w1", w1_raw_words, t, nc.gpsimd) for t in range(1, PACK))
+        w2_dealt_scales = deal_scales("w2", w2_raw_scales, nc.vector)
+        w2_dealt_words = [deal_words("w2", w2_raw_words, t, nc.vector) for t in range(PACK)]
 
-        def product(weight, h, tag, bufs):
-            words, scales = weight
+        def product(words, scales, h, tag, bufs):
             acc = psum.tile([P, BANK], F32, name=tag, tag=tag, bufs=bufs)
             for o in range(PASSES):
                 nc.tensor.matmul_mx(
                     out=acc[:],
                     lhsT=words[:, o].rearrange("p m b -> p (m b)").bitcast(FP4X4),
                     lhsT_scale=scales[:, o, :],
-                    rhs=xw[o, h][:].bitcast(FP8X4),
-                    rhs_scale=xs[o][:, h * BANK : (h + 1) * BANK],
+                    rhs=picked_words[o, h][:].bitcast(FP8X4),
+                    rhs_scale=picked_scales[o][:, date_half(h)],
                     start=(o == 0),
                     stop=(o == PASSES - 1),
                 )
             return acc
-
 
         unit7 = keep.tile([P, PACK], F32, name="unit7")
         nc.vector.tensor_scalar(unit7[:], unit_sb[:], 0.7, None, ALU.mult)
@@ -162,105 +162,86 @@ def tile_picked_ydeepm_loss_p_kernel(
         gain = [keep.tile([P, S], F32, name="gain%d" % t) for t in range(PACK)]
         for t in range(PACK):
             nc.vector.memset(neg_term[t][:, V:], 0.0)
-
-        def positions(t, h):
-            dl = product(w1[t], h, "dl", 4)
-            nc.scalar.activation(pos[t][:, h * BANK : (h + 1) * BANK], dl[:], ACT.Tanh)
-
         ident = keep.tile([P, P], F32, name="ident")
         make_identity(nc, ident[:])
-        back = {}
-
-        def gains(t, h):
-            dates = slice(h * BANK, (h + 1) * BANK)
-            ds = product(w2[t], h, "ds", 2)
-            if t not in (2,3):
-                nc.vector.tensor_tensor(gain[t][:, dates], ds[:], pos[t][:, dates], ALU.mult)
-                return
-            order = "p (v e d) -> p e v d"
-            nc.vector.tensor_tensor(
-                gain[t][:, dates].rearrange("p (e v d) -> p e v d", e=2, d=2),
-                ds[:].rearrange(order, e=2, d=2), pos[t][:, dates].rearrange(order, e=2, d=2), ALU.mult,
-            )
-
-        def gain_sums(t, copier):
-            if t not in (2,3):
-                back[t] = keep.tile([P, V], F32, name="back%d" % t)
-                nc.vector.tensor_reduce(back[t][:], gain[t][:].rearrange("p (v d) -> p v d", d=D), AXIS_X, ALU.add)
-                return
-            bank = psum.tile([P, 2, DATE_HALVES, P], F32, name="turned", tag="turned", bufs=2)
-            turned = bank[:, 0]
-            for h in range(DATE_HALVES):
-                planes = gain[t][:, h * BANK : (h + 1) * BANK].rearrange("p (e v d) -> p e d v", e=2, d=2)
-                for j in range(D):
-                    nc.tensor.matmul(turned[:, h, :], planes[:, j // 2, j % 2, :], ident[:],
-                                     start=(j == 0), stop=(j == D - 1), is_transpose=True)
-            turned_sb = work.tile([P, DATE_HALVES, P], F32, name="turned_sb", bufs=2)
-            copier(turned_sb[:], turned)
-            back[t] = bank[:, 1].rearrange("p h v -> p (h v)")
-            for h in range(DATE_HALVES):
-                nc.tensor.transpose(back[t][:, h * P : (h + 1) * P], turned_sb[:, h, :], ident[:])
-
         dp = [keep.tile([P, S], F32, name="dp%d" % t) for t in range(PACK)]
-
-        def gather(on_scalar, dst, src):
-            if on_scalar:
-                nc.scalar.activation(dst, src, ACT.Copy)
-            else:
-                nc.vector.tensor_copy(dst, src)
-
-        def previous(t, a, b, on_scalar):
-            gather(on_scalar, dp[t][:, a:b], pos[t][:].indirect(prv_sb[:, a // LIST_COL : b // LIST_COL]))
-
-        def trades(t, a, b, engine):
-            engine.tensor_tensor(trade[t][:, a:b], pos[t][:, a:b], dp[t][:, a:b], ALU.subtract)
-
-        sums = [keep.tile([P, V], F32, name="trade_sum%d" % t) for t in range(4)]
-        trade_sum = [sums[i] for i in (0,1,2,3)]
-
-        def trade_sums(t, a, b):
-            nc.vector.tensor_reduce(
-                trade_sum[t][:, a // D : b // D], trade[t][:, a:b].rearrange("p (v d) -> p v d", d=D), AXIS_X, ALU.add,
-                apply_absolute_value=True,
-            )
-
-        def terms(t, a, b):
-            nc.vector.scalar_tensor_tensor(
-                neg_term[t][:, a // D : b // D],
-                trade_sum[t][:, a // D : b // D], 0.4, back[t][:, a // D : b // D], ALU.mult, ALU.subtract,
-            )
-
+        trade_sum = [keep.tile([P, V], F32, name="trade_sum%d" % t) for t in range(PACK)]
+        gain_sum = {}
         neg_tpp = [keep.tile([P, U], F32, name="neg_tpp%d" % t) for t in range(PACK)]
         neg_net = [keep.tile([P, U], F32, name="neg_net%d" % t) for t in range(PACK)]
         risk = [keep.tile([P, U], F32, name="risk%d" % t) for t in range(PACK)]
         hid = keep.tile([P, PACK, U], BF16, name="hid")
 
-        def paths(t, a, b, on_scalar):
-            gather(on_scalar, neg_tpp[t][:, a:b], neg_term[t][:].indirect(path_sb[:, a // LIST_COL : b // LIST_COL]))
+        def positions(t):
+            for h in range(DATE_HALVES):
+                dl = product(w1_dealt_words[t], w1_dealt_scales[:, :, t, :], h, "dl", DL_BANKS)
+                nc.scalar.activation(pos[t][:, date_half(h)], dl[:], ACT.Tanh)
 
-        def nets(t, a, b, engine):
-            engine.tensor_tensor(neg_net[t][:, a:b], neg_tpp[t][:, a:b], clm_sb[:, t, a:b], ALU.add)
+        def previous(t, h):
+            return pos[t][:].indirect(entries(prv_sb, h * BANK, (h + 1) * BANK))
 
-        def path_nets(t, a, b):
-            nc.vector.tensor_tensor(
-                neg_net[t][:, a:b], neg_term[t][:].indirect(path_sb[:, a // LIST_COL : b // LIST_COL]),
-                clm_sb[:, t, a:b], ALU.add,
+        def trades(t, h, engine):
+            engine.tensor_tensor(trade[t][:, date_half(h)], pos[t][:, date_half(h)], dp[t][:, date_half(h)], ALU.subtract)
+
+        def gains(t):
+            for h in range(DATE_HALVES):
+                ds = product(w2_dealt_words[t], w2_dealt_scales[:, :, t, :], h, "ds", DS_BANKS)
+                if t == 0:
+                    nc.vector.tensor_tensor(gain[t][:, date_half(h)], ds[:], pos[t][:, date_half(h)], ALU.mult)
+                else:
+                    by_pairs = "p (v e d) -> p e v d"
+                    nc.vector.tensor_tensor(
+                        gain[t][:, date_half(h)].rearrange("p (e v d) -> p e v d", e=2, d=2),
+                        ds[:].rearrange(by_pairs, e=2, d=2),
+                        pos[t][:, date_half(h)].rearrange(by_pairs, e=2, d=2),
+                        ALU.mult,
+                    )
+
+        def gain_sums(t):
+            if t == 0:
+                gain_sum[t] = keep.tile([P, V], F32, name="gain_sum0")
+                nc.vector.tensor_reduce(gain_sum[t][:], gain[t][:].rearrange("p (v d) -> p v d", d=D), AXIS_X, ALU.add)
+                return
+            bank = psum.tile([P, 2, DATE_HALVES, P], F32, name="sums", tag="sums", bufs=SUM_BANKS)
+            turned = bank[:, 0]
+            for h in range(DATE_HALVES):
+                runs = gain[t][:, date_half(h)].rearrange("p (e v d) -> p e d v", e=2, d=2)
+                for j in range(D):
+                    nc.tensor.matmul(
+                        turned[:, h, :], runs[:, j // 2, j % 2, :], ident[:],
+                        start=(j == 0), stop=(j == D - 1), is_transpose=True,
+                    )
+            turned_sb = work.tile([P, DATE_HALVES, P], F32, name="turned_sb")
+            nc.vector.tensor_copy(turned_sb[:], turned)
+            gain_sum[t] = bank[:, 1].rearrange("p h v -> p (h v)")
+            for h in range(DATE_HALVES):
+                nc.tensor.transpose(gain_sum[t][:, h * P : (h + 1) * P], turned_sb[:, h, :], ident[:])
+
+        def trade_sums(t, a, b):
+            nc.vector.tensor_reduce(
+                trade_sum[t][:, a // D : b // D], trade[t][:, a:b].rearrange("p (v d) -> p v d", d=D),
+                AXIS_X, ALU.add, apply_absolute_value=True,
             )
+
+        def terms(t):
+            nc.vector.scalar_tensor_tensor(
+                neg_term[t][:, :V], trade_sum[t][:], 0.4, gain_sum[t][:, :V], ALU.mult, ALU.subtract
+            )
+
+        def paths(t):
+            for a in (0, CLAIM_HALF):
+                b = a + CLAIM_HALF
+                nc.scalar.activation(neg_tpp[t][:, a:b], neg_term[t][:].indirect(entries(path_sb, a, b)), ACT.Copy)
+
+        def nets(t, a, b):
+            nc.vector.tensor_tensor(neg_net[t][:, a:b], neg_tpp[t][:, a:b], clm_sb[:, t, a:b], ALU.add)
 
         def risks(t, a, b):
             nc.vector.scalar_tensor_tensor(
                 risk[t][:, a:b], neg_net[t][:, a:b], -0.3 / 0.7, neg_net[t][:, a:b], ALU.mult, ALU.max
             )
 
-        def hidden(t, a, b, engine):
-            if engine == "S":
-                nc.scalar.activation(hid[:, t, a:b], risk[t][:, a:b], ACT.Copy, scale=unit7[:, t : t + 1])
-            elif engine == "G":
-                nc.gpsimd.tensor_scalar(hid[:, t, a:b], risk[t][:, a:b], unit7[:, t : t + 1], 0.0, ALU.mult, ALU.add)
-            else:
-                nc.vector.tensor_scalar(hid[:, t, a:b], risk[t][:, a:b], unit7[:, t : t + 1], None, ALU.mult)
-
-        def result(a, b, copier):
+        def result(a, b, copy_out):
             n = b - a
             woven = keep.tile([P, n, PACK], BF16, name="woven%d" % a, align_bytes=64)
             nc.vector.tensor_copy(
@@ -272,65 +253,53 @@ def tile_picked_ydeepm_loss_p_kernel(
             nc.vector.quantize_mx(
                 out=codes[:].bitcast(FP8X4), scales=scales[:], in_=woven[:].rearrange("p c t -> p (c t)")
             )
-            acc = psum.tile([P, n], F32, name="res", tag="dl", bufs=4)
+            acc = psum.tile([P, n], F32, name="res", tag="dl", bufs=DL_BANKS)
             nc.tensor.matmul_mx(
-                out=acc[:], lhsT=w3w[:].bitcast(FP4X4), lhsT_scale=w3s[:],
+                out=acc[:], lhsT=w3_words_sb[:].bitcast(FP4X4), lhsT_scale=w3_scales_sb[:],
                 rhs=codes[:].bitcast(FP8X4), rhs_scale=scales[:], start=True, stop=True,
             )
             res = keep.tile([P, n], F32, name="res_sb%d" % a)
-            copier(res[:], acc[:])
+            copy_out(res[:], acc[:])
             nc.sync.dma_start(out[:, a:b], res[:])
 
-        G = nc.gpsimd
-        LAST = PACK - 1
-        def both(step, t):
-            step(t, 0)
-            step(t, 1)
-        def claims(t):
-            paths(t, 0, 256, (False,True,True)[t])
-            paths(t, 256, 512, True)
-            nets(t, 0, 512, (G,G,nc.vector)[t])
-        def finish(t):
-            risks(t, 0, 512)
-            hidden(t, 0, 512, "SSS"[t])
-        both(positions, 0)
-        previous(0, 0, 512, False)
-        previous(0, 512, 1024, True)
-        both(positions, 1)
-        both(gains, 0)
+        positions(0)
+        nc.vector.tensor_copy(dp[0][:, date_half(0)], previous(0, 0))
+        nc.scalar.activation(dp[0][:, date_half(1)], previous(0, 1), ACT.Copy)
+        positions(1)
+        gains(0)
         for t in range(LAST):
-            trades(t, 0, 512, G)
-            trades(t, 512, 1024, G)
-            both(gains, t + 1)
-            gain_sums(t, nc.scalar.copy)
-            trade_sums(t, 0, 1024)
-            terms(t, 0, 1024)
-            previous(t + 1, 0, 512, True)
-            previous(t + 1, 512, 1024, True)
+            for h in range(DATE_HALVES):
+                nc.scalar.activation(dp[t + 1][:, date_half(h)], previous(t + 1, h), ACT.Copy)
             if t + 2 < PACK:
-                both(positions, t + 2)
-            if t >= 0:
-                claims(t - 0)
-            if t >= 3:
-                finish(t - 3)
-        gain_sums(LAST, nc.scalar.copy)
-        trades(LAST, 0, 512, G)
-        trades(LAST, 512, 1024, G)
-        trade_sums(LAST, 0, 512)
-        trade_sums(LAST, 512, 1024)
-        terms(LAST, 0, 1024)
-        for t in range(max(0, LAST - 0), LAST):
-            claims(t)
-        paths(LAST, 0, 256, True)
-        paths(LAST, 256, 512, True)
-        for t in range(max(0, LAST - 3), LAST):
-            finish(t)
-        for c in range(2):
-            nets(LAST, 256 * c, 256 * c + 256, nc.vector)
-            risks(LAST, 256 * c, 256 * c + 256)
-            hidden(LAST, 256 * c, 256 * c + 256, "V")
-            if c == 0:
-                result(0, 256, nc.scalar.copy)
-            else:
-                result(256, 384, nc.scalar.copy)
-                result(384, 512, nc.vector.tensor_copy)
+                positions(t + 2)
+            for h in range(DATE_HALVES):
+                trades(t, h, nc.gpsimd)
+            gains(t + 1)
+            gain_sums(t)
+            trade_sums(t, 0, S)
+            terms(t)
+        gain_sums(LAST)
+        trades(LAST, 0, nc.gpsimd)
+        trades(LAST, 1, nc.vector)
+        for h in range(DATE_HALVES):
+            trade_sums(LAST, h * BANK, (h + 1) * BANK)
+        terms(LAST)
+
+        for t in range(LAST):
+            paths(t)
+            nets(t, 0, U)
+        paths(LAST)
+        for t in range(LAST):
+            risks(t, 0, U)
+            nc.scalar.activation(hid[:, t, :], risk[t][:], ACT.Copy, scale=unit7[:, t : t + 1])
+
+        def last_hidden(a, b):
+            nets(LAST, a, b)
+            risks(LAST, a, b)
+            nc.vector.tensor_scalar(hid[:, LAST, a:b], risk[LAST][:, a:b], unit7[:, LAST:], None, ALU.mult)
+
+        last_hidden(0, CLAIM_HALF)
+        result(0, CLAIM_HALF, nc.scalar.copy)
+        last_hidden(CLAIM_HALF, U)
+        result(CLAIM_HALF, U - CLAIM_QUARTER, nc.scalar.copy)
+        result(U - CLAIM_QUARTER, U, nc.vector.tensor_copy)

from contextlib import ExitStack

import concourse.mybir as mybir
from concourse.masks import make_identity

K, T, S, D, N, H, V, U = 1024, 2048, 1024, 4, 128, 512, 256, 512
FLOPS = 2 * (2 * K * H * S + H * N * U)

F32 = mybir.dt.float32
BF16 = mybir.dt.bfloat16
I32 = mybir.dt.int32
U32 = mybir.dt.uint32
U16 = mybir.dt.uint16
U8 = mybir.dt.uint8
FP8X4 = mybir.dt.float8_e4m3fn_x4
FP4X4 = mybir.dt.float4_e2m1fn_x4
ALU = mybir.AluOpType
ACT = mybir.ActivationFunctionType
AXIS_X = mybir.AxisListType.X

P = 128
PACK = 4
PASSES = K // (P * PACK)
QUADRANTS = 4
BANK = 512
DATE_HALVES = S // BANK
CLAIM_HALF = U // 2
CLAIM_QUARTER = U // 4
LIST_COL = 16
TERM_WINDOW = V + 32
SHIFT_ROWS = 112
LAST = PACK - 1

DL_BANKS, DS_BANKS, SUM_BANKS = 4, 2, 2


def tile_picked_ydeepm_loss_p_kernel(
    tc, x_words, x_scales, w1_words, w1_scales, w2_words, w2_scales, clm, unit,
    w3_words, w3_scales, offs, prv, path, out,
):
    nc = tc.nc
    with ExitStack() as ctx:
        keep = ctx.enter_context(tc.tile_pool(name="keep", bufs=1))
        work = ctx.enter_context(tc.tile_pool(name="work", bufs=2))
        psum = ctx.enter_context(tc.psum_pool(name="psum", bufs=1))

        def entries(list_tile, a, b):
            return list_tile[:, a // LIST_COL : b // LIST_COL]

        def date_half(h):
            return slice(h * BANK, (h + 1) * BANK)

        offs_sb = keep.tile([P, S // LIST_COL], U16, name="offs_sb")
        prv_sb = keep.tile([P, S // LIST_COL], U16, name="prv_sb")
        path_sb = keep.tile([P, U // LIST_COL], U16, name="path_sb")

        x_scale_table = keep.tile([P, T], U8, name="x_scale_table", align_bytes=64)
        nc.gpsimd.memset(x_scale_table[:].bitcast(I32), 0)
        w1_raw_words = keep.tile([P, PASSES, 2 * H], U8, name="w1_raw_words")
        w1_raw_scales = keep.tile([P, PASSES, H], U8, name="w1_raw_scales")
        w2_raw_words = keep.tile([P, PASSES, 2 * H], U8, name="w2_raw_words")
        w2_raw_scales = keep.tile([P, PASSES, H], U8, name="w2_raw_scales")

        def load_x_words(o):
            table = keep.tile([P, T], I32, name="x_word_table%d" % o, align_bytes=64)
            nc.sync.dma_start(table[:], x_words[o].rearrange("p c r -> p (c r)").bitcast(I32))
            return table

        def load_weight_words(raw_words, words):
            nc.sync.dma_start(raw_words[:].bitcast(I32), words.rearrange("o p c -> p o c").bitcast(I32))

        def load_weight_scales(raw_scales, scales):
            nc.vector.memset(raw_scales[:].rearrange("p o c -> p (o c)").bitcast(I32), 0)
            for q in range(QUADRANTS):
                nc.sync.dma_start(
                    raw_scales[32 * q : 32 * q + 4].bitcast(I32),
                    scales[:, 4 * q : 4 * q + 4, :].rearrange("o r c -> r o c").bitcast(I32),
                )

        nc.sync.dma_start(offs_sb[:], offs)
        load_weight_words(w1_raw_words, w1_words)
        nc.sync.dma_start(prv_sb[:], prv)
        for q in range(QUADRANTS):
            nc.sync.dma_start(
                x_scale_table[32 * q : 32 * q + 8, :].bitcast(I32),
                x_scales[:, 4 * q : 4 * q + 4, :].bitcast(I32),
            )
        x_word_tables = [load_x_words(0)]
        load_weight_scales(w1_raw_scales, w1_scales)
        x_word_tables.append(load_x_words(1))
        load_weight_scales(w2_raw_scales, w2_scales)
        load_weight_words(w2_raw_words, w2_words)
        nc.sync.dma_start(path_sb[:], path)
        unit_sb = keep.tile([P, PACK], F32, name="unit_sb")
        nc.sync.dma_start(unit_sb[:], unit.rearrange("(p t) one -> p (t one)", t=PACK))
        clm_sb = keep.tile([P, PACK, U], F32, name="clm_sb")
        nc.sync.dma_start(clm_sb[:], clm.rearrange("(p t) r -> p t r", t=PACK))
        w3_words_sb = keep.tile([P, 2 * N], U8, name="w3_words_sb", align_bytes=64)
        nc.sync.dma_start(w3_words_sb[:].bitcast(I32), w3_words[0].bitcast(I32))
        w3_scales_sb = keep.tile([P, N], U8, name="w3_scales_sb", align_bytes=64)
        nc.vector.memset(w3_scales_sb[:].bitcast(I32), 0)
        for q in range(QUADRANTS):
            nc.sync.dma_start(
                w3_scales_sb[32 * q : 32 * q + 4, :].bitcast(I32),
                w3_scales[0, 4 * q : 4 * q + 4, :].bitcast(I32),
            )

        picked_scales0 = keep.tile([P, S], U8, name="picked_scales0", align_bytes=64)
        nc.vector.tensor_copy(picked_scales0[:], x_scale_table[:].indirect(offs_sb[:]))
        picked_scales1 = keep.tile([P, S], U8, name="picked_scales1", align_bytes=64)
        nc.vector.memset(picked_scales1[:].bitcast(I32), 0)
        nc.scalar.dma_start(
            picked_scales1[0:SHIFT_ROWS, :].bitcast(I32), picked_scales0[4 : 4 + SHIFT_ROWS, :].bitcast(I32)
        )
        picked_scales = [picked_scales0, picked_scales1]
        picked_words = {}
        for o in range(PASSES):
            for h in range(DATE_HALVES):
                picked = keep.tile([P, BANK], U32, name="picked_words%d%d" % (o, h), align_bytes=64)
                table = x_word_tables[o][:].bitcast(U32)
                nc.vector.tensor_copy(picked[:], table.indirect(entries(offs_sb, h * BANK, (h + 1) * BANK)))
                picked_words[o, h] = picked

        def deal_words(name, raw_words, t, engine):
            words = keep.tile([P, PASSES, P, 2], U8, name="%s_words%d" % (name, t), align_bytes=64)
            columns = raw_words[:].rearrange("p o (m t b) -> p o m t b", t=PACK, b=2)
            engine.tensor_copy(words[:], columns[:, :, :, t, :])
            return words

        def deal_scales(name, raw_scales, engine):
            scales = keep.tile([P, PASSES, PACK, P], U8, name="%s_scales" % name, align_bytes=64)
            columns = raw_scales[:].rearrange("p o (m t) -> p o t m", t=PACK)
            for a, b in ((0, 1), (1, PACK)):
                engine.tensor_copy(scales[:, :, a:b, :], columns[:, :, a:b, :])
            return scales

        w1_dealt_words = [deal_words("w1", w1_raw_words, 0, nc.gpsimd)]
        w1_dealt_scales = deal_scales("w1", w1_raw_scales, nc.gpsimd)
        w1_dealt_words.extend(deal_words("w1", w1_raw_words, t, nc.gpsimd) for t in range(1, PACK))
        w2_dealt_scales = deal_scales("w2", w2_raw_scales, nc.vector)
        w2_dealt_words = [deal_words("w2", w2_raw_words, t, nc.vector) for t in range(PACK)]

        def product(words, scales, h, tag, bufs):
            acc = psum.tile([P, BANK], F32, name=tag, tag=tag, bufs=bufs)
            for o in range(PASSES):
                nc.tensor.matmul_mx(
                    out=acc[:],
                    lhsT=words[:, o].rearrange("p m b -> p (m b)").bitcast(FP4X4),
                    lhsT_scale=scales[:, o, :],
                    rhs=picked_words[o, h][:].bitcast(FP8X4),
                    rhs_scale=picked_scales[o][:, date_half(h)],
                    start=(o == 0),
                    stop=(o == PASSES - 1),
                )
            return acc

        unit7 = keep.tile([P, PACK], F32, name="unit7")
        nc.vector.tensor_scalar(unit7[:], unit_sb[:], 0.7, None, ALU.mult)
        pos = [keep.tile([P, S], F32, name="pos%d" % t) for t in range(PACK)]
        neg_term = [keep.tile([P, TERM_WINDOW], F32, name="neg_term%d" % t) for t in range(PACK)]
        trade = [keep.tile([P, S], F32, name="trade%d" % t) for t in range(PACK)]
        gain = [keep.tile([P, S], F32, name="gain%d" % t) for t in range(PACK)]
        for t in range(PACK):
            nc.vector.memset(neg_term[t][:, V:], 0.0)
        ident = keep.tile([P, P], F32, name="ident")
        make_identity(nc, ident[:])
        dp = [keep.tile([P, S], F32, name="dp%d" % t) for t in range(PACK)]
        trade_sum = [keep.tile([P, V], F32, name="trade_sum%d" % t) for t in range(PACK)]
        gain_sum = {}
        neg_tpp = [keep.tile([P, U], F32, name="neg_tpp%d" % t) for t in range(PACK)]
        neg_net = [keep.tile([P, U], F32, name="neg_net%d" % t) for t in range(PACK)]
        risk = [keep.tile([P, U], F32, name="risk%d" % t) for t in range(PACK)]
        hid = keep.tile([P, PACK, U], BF16, name="hid")

        def positions(t):
            for h in range(DATE_HALVES):
                dl = product(w1_dealt_words[t], w1_dealt_scales[:, :, t, :], h, "dl", DL_BANKS)
                nc.scalar.activation(pos[t][:, date_half(h)], dl[:], ACT.Tanh)

        def previous(t, h):
            return pos[t][:].indirect(entries(prv_sb, h * BANK, (h + 1) * BANK))

        def trades(t, h, engine):
            engine.tensor_tensor(trade[t][:, date_half(h)], pos[t][:, date_half(h)], dp[t][:, date_half(h)], ALU.subtract)

        def gains(t):
            for h in range(DATE_HALVES):
                ds = product(w2_dealt_words[t], w2_dealt_scales[:, :, t, :], h, "ds", DS_BANKS)
                if t == 0:
                    nc.vector.tensor_tensor(gain[t][:, date_half(h)], ds[:], pos[t][:, date_half(h)], ALU.mult)
                else:
                    by_pairs = "p (v e d) -> p e v d"
                    nc.vector.tensor_tensor(
                        gain[t][:, date_half(h)].rearrange("p (e v d) -> p e v d", e=2, d=2),
                        ds[:].rearrange(by_pairs, e=2, d=2),
                        pos[t][:, date_half(h)].rearrange(by_pairs, e=2, d=2),
                        ALU.mult,
                    )

        def gain_sums(t):
            if t == 0:
                gain_sum[t] = keep.tile([P, V], F32, name="gain_sum0")
                nc.vector.tensor_reduce(gain_sum[t][:], gain[t][:].rearrange("p (v d) -> p v d", d=D), AXIS_X, ALU.add)
                return
            bank = psum.tile([P, 2, DATE_HALVES, P], F32, name="sums", tag="sums", bufs=SUM_BANKS)
            turned = bank[:, 0]
            for h in range(DATE_HALVES):
                runs = gain[t][:, date_half(h)].rearrange("p (e v d) -> p e d v", e=2, d=2)
                for j in range(D):
                    nc.tensor.matmul(
                        turned[:, h, :], runs[:, j // 2, j % 2, :], ident[:],
                        start=(j == 0), stop=(j == D - 1), is_transpose=True,
                    )
            turned_sb = work.tile([P, DATE_HALVES, P], F32, name="turned_sb")
            nc.vector.tensor_copy(turned_sb[:], turned)
            gain_sum[t] = bank[:, 1].rearrange("p h v -> p (h v)")
            for h in range(DATE_HALVES):
                nc.tensor.transpose(gain_sum[t][:, h * P : (h + 1) * P], turned_sb[:, h, :], ident[:])

        def trade_sums(t, a, b):
            nc.vector.tensor_reduce(
                trade_sum[t][:, a // D : b // D], trade[t][:, a:b].rearrange("p (v d) -> p v d", d=D),
                AXIS_X, ALU.add, apply_absolute_value=True,
            )

        def terms(t):
            nc.vector.scalar_tensor_tensor(
                neg_term[t][:, :V], trade_sum[t][:], 0.4, gain_sum[t][:, :V], ALU.mult, ALU.subtract
            )

        def paths(t):
            for a in (0, CLAIM_HALF):
                b = a + CLAIM_HALF
                nc.scalar.activation(neg_tpp[t][:, a:b], neg_term[t][:].indirect(entries(path_sb, a, b)), ACT.Copy)

        def nets(t, a, b):
            nc.vector.tensor_tensor(neg_net[t][:, a:b], neg_tpp[t][:, a:b], clm_sb[:, t, a:b], ALU.add)

        def risks(t, a, b):
            nc.vector.scalar_tensor_tensor(
                risk[t][:, a:b], neg_net[t][:, a:b], -0.3 / 0.7, neg_net[t][:, a:b], ALU.mult, ALU.max
            )

        def result(a, b, copy_out):
            n = b - a
            woven = keep.tile([P, n, PACK], BF16, name="woven%d" % a, align_bytes=64)
            nc.vector.tensor_copy(
                woven[:].rearrange("p (c i) t -> p c t i", i=4),
                hid[:, :, a:b].rearrange("p t (c i) -> p c t i", i=4),
            )
            codes = keep.tile([P, n], U32, name="codes%d" % a, align_bytes=64)
            scales = keep.tile([P, n], U8, name="scales%d" % a, align_bytes=64)
            nc.vector.quantize_mx(
                out=codes[:].bitcast(FP8X4), scales=scales[:], in_=woven[:].rearrange("p c t -> p (c t)")
            )
            acc = psum.tile([P, n], F32, name="res", tag="dl", bufs=DL_BANKS)
            nc.tensor.matmul_mx(
                out=acc[:], lhsT=w3_words_sb[:].bitcast(FP4X4), lhsT_scale=w3_scales_sb[:],
                rhs=codes[:].bitcast(FP8X4), rhs_scale=scales[:], start=True, stop=True,
            )
            res = keep.tile([P, n], F32, name="res_sb%d" % a)
            copy_out(res[:], acc[:])
            nc.sync.dma_start(out[:, a:b], res[:])

        positions(0)
        nc.vector.tensor_copy(dp[0][:, date_half(0)], previous(0, 0))
        nc.scalar.activation(dp[0][:, date_half(1)], previous(0, 1), ACT.Copy)
        positions(1)
        gains(0)
        for t in range(LAST):
            for h in range(DATE_HALVES):
                nc.scalar.activation(dp[t + 1][:, date_half(h)], previous(t + 1, h), ACT.Copy)
            if t + 2 < PACK:
                positions(t + 2)
            for h in range(DATE_HALVES):
                trades(t, h, nc.gpsimd)
            gains(t + 1)
            gain_sums(t)
            trade_sums(t, 0, S)
            terms(t)
        gain_sums(LAST)
        trades(LAST, 0, nc.gpsimd)
        trades(LAST, 1, nc.vector)
        for h in range(DATE_HALVES):
            trade_sums(LAST, h * BANK, (h + 1) * BANK)
        terms(LAST)

        for t in range(LAST):
            paths(t)
            nets(t, 0, U)
        paths(LAST)
        for t in range(LAST):
            risks(t, 0, U)
            nc.scalar.activation(hid[:, t, :], risk[t][:], ACT.Copy, scale=unit7[:, t : t + 1])

        def last_hidden(a, b):
            nets(LAST, a, b)
            risks(LAST, a, b)
            nc.vector.tensor_scalar(hid[:, LAST, a:b], risk[LAST][:, a:b], unit7[:, LAST:], None, ALU.mult)

        last_hidden(0, CLAIM_HALF)
        result(0, CLAIM_HALF, nc.scalar.copy)
        last_hidden(CLAIM_HALF, U)
        result(CLAIM_HALF, U - CLAIM_QUARTER, nc.scalar.copy)
        result(U - CLAIM_QUARTER, U, nc.vector.tensor_copy)
